import numpy as np
import ml_dtypes


def mxq(x, axis, fmt="e4m3"):
    dtype, down = {"e4m3": (ml_dtypes.float8_e4m3fn, 7), "e5m2": (ml_dtypes.float8_e5m2, 14)}[fmt]
    v = np.moveaxis(np.asarray(x, np.float32).astype(ml_dtypes.bfloat16).astype(np.float64), axis, -1)
    blocks = v.reshape(v.shape[:-1] + (-1, 32))
    amax = np.abs(blocks).max(-1, keepdims=True)
    byte = np.maximum(np.where(amax > 0, np.frexp(amax)[1] - 1 + 127, 0) - down, 1)
    scale = np.exp2(byte - 127.0)
    codes = (blocks / scale).astype(np.float32).astype(dtype).astype(np.float64)
    return np.moveaxis((codes * scale).reshape(v.shape), -1, axis)


WIDE = False


def mx_kscale(k):
    if not WIDE:
        return np.ones(k)
    levels = np.array([10, -10, 5, -5, 0])
    if k % 512:
        return np.exp2(np.random.permutation(np.resize(levels, k // 32))).repeat(32)
    a = np.empty((k // 512, 16))
    for p in range(k // 512):
        a[p, :8] = np.random.permutation(np.resize(levels, 8))
        for g in range(8):
            far = levels[np.abs(levels - a[p, g]) >= 10]
            a[p, g + 8] = far[np.random.randint(len(far))]
    return np.exp2(a.ravel()).repeat(32)


def f64(x):
    return np.asarray(x).astype(np.float64)


def striped(idx):
    return np.tile(np.asarray(idx).reshape(-1, 16).T, (8, 1)).astype(np.uint16)


def unstriped(offs):
    return offs[:16].T.reshape(-1).astype(np.int64)


E2M1 = np.array([0.0, 0.5, 1.0, 1.5, 2.0, 3.0, 4.0, 6.0, -0.0, -0.5, -1.0, -1.5, -2.0, -3.0, -4.0, -6.0])


def pack_weight(w, fmt):
    k, n = w.shape
    w = f64(np.asarray(w, np.float32).astype(ml_dtypes.bfloat16)).reshape(k // 32, 32, n)
    amax = np.abs(w).max(1)
    if fmt == "e4m3":
        byte = np.frexp(amax)[1] - 1 + 127 - 7
    else:
        mant, ex = np.frexp(amax / 6.0)
        byte = np.where(mant > 0.5, ex, ex - 1) + 127
    byte = np.clip(np.where(amax > 0, byte, 1), 1, 254)
    scaled = (w * np.exp2(127.0 - byte)[:, None, :]).reshape(k, n).astype(np.float32)
    by_word = np.ascontiguousarray(scaled.reshape(k // 512, 128, 4, n).transpose(0, 1, 3, 2))
    if fmt == "e4m3":
        words = by_word.astype(ml_dtypes.float8_e4m3fn).view(np.uint8)
    else:
        c = by_word.astype(ml_dtypes.float4_e2m1fn).view(np.uint8) & 0xF
        words = (c[..., 0::2] | (c[..., 1::2] << 4)).reshape(k // 512, 128, 2 * n)
    return np.ascontiguousarray(words), np.ascontiguousarray(byte.astype(np.uint8).reshape(k // 512, 16, n))


def unpack_weight(words, scales, fmt):
    g, _, n = scales.shape
    words = np.ascontiguousarray(words).reshape(g, 128, n, -1)
    if fmt == "e4m3":
        vals = words.view(ml_dtypes.float8_e4m3fn).astype(np.float64)
    else:
        nib = np.empty((g, 128, n, 4), np.uint8)
        nib[..., 0::2] = words & 0xF
        nib[..., 1::2] = words >> 4
        vals = E2M1[nib]
    vals = vals * np.repeat(np.exp2(scales.astype(np.float64) - 127.0), 8, axis=1)[..., None]
    return vals.transpose(0, 1, 3, 2).reshape(g * 512, n)


def sigmoid(v):
    return 1.0 / (1.0 + np.exp(-v))


def bf(x):
    return np.asarray(x, np.float32).astype(ml_dtypes.bfloat16)


def planes(Y):
    r, m = Y.shape
    b = f64(bf(Y)).reshape(r // 32, 32, m)
    amax = np.abs(b).max(1)
    byte = np.clip(np.where(amax > 0, np.frexp(amax)[1] - 1 + 127 - 7, 1), 1, 254)
    codes = (b * np.exp2(127.0 - byte)[:, None, :]).reshape(r, m).astype(np.float32).astype(ml_dtypes.float8_e4m3fn).view(np.uint8)
    words = codes.reshape(r // 512, 128, 4, m).transpose(0, 1, 3, 2)
    return np.ascontiguousarray(words), np.ascontiguousarray(byte.astype(np.uint8).reshape(r // 512, 16, m))


K, T, J, R, N = 1024, 1024, 512, 512, 512


def setup_inputs():
    n = np.random.standard_normal
    idx = np.random.permutation(T)[:J]
    idx2 = np.random.permutation(T)[:J]
    fk = mx_kscale(K)
    fr = mx_kscale(R)
    xtp = pack_weight(n((K, T)) / fk[:, None], "e2m1")
    wap = pack_weight(n((K, R)) * 1 / np.sqrt(K) * fk[:, None], "e4m3")
    wcp = pack_weight(n((K, R)) * 1 / np.sqrt(K) * fk[:, None], "e2m1")
    wgp = pack_weight(n((K, R)) * 1 / np.sqrt(K) * fk[:, None], "e4m3")
    wbp = pack_weight(n((R, N)) * 1 / np.sqrt(R) / fr[:, None], "e2m1")
    return {
        "xt_words": xtp[0],
        "xt_scales": xtp[1],
        "wa_words": wap[0],
        "wa_scales": wap[1],
        "wc_words": wcp[0],
        "wc_scales": wcp[1],
        "wg_words": wgp[0],
        "wg_scales": wgp[1],
        "us": (np.random.uniform(0.5, 2.0, (R, 1)) * fr[:, None]).astype(np.float32),
        "wb_words": wbp[0],
        "wb_scales": wbp[1],
        "rw": (np.random.uniform(0.5, 2.0, (1, J))).astype(np.float32),
        "offs": striped(idx),
        "offs2": striped(idx2),
    }


def reference(xt_words, xt_scales, wa_words, wa_scales, wc_words, wc_scales, wg_words, wg_scales, us, wb_words, wb_scales, rw, offs, offs2):
    idx = unstriped(offs)
    idx2 = unstriped(offs2)
    xtu = unpack_weight(xt_words, xt_scales, "e2m1")
    wau = unpack_weight(wa_words, wa_scales, "e4m3")
    wcu = unpack_weight(wc_words, wc_scales, "e2m1")
    wgu = unpack_weight(wg_words, wg_scales, "e4m3")
    wbu = unpack_weight(wb_words, wb_scales, "e2m1")
    xtidxg = xtu[:, idx]
    a = wau.T @ xtidxg
    xtidx2g = xtu[:, idx2]
    b = wcu.T @ xtidx2g
    g = wgu.T @ xtidxg
    hid = (b + sigmoid(g) * (a - b)) * f64(us)
    hidq = mxq(hid, 0, "e4m3")
    p = wbu.T @ hidq
    y = p * f64(rw)
    words, scales = planes(y)
    return y, words, scales

@@ -1,0 +1,281 @@
+from contextlib import ExitStack
+
+import concourse.mybir as mybir
+from concourse.masks import make_identity
+
+K, T, J, R, N = 1024, 1024, 512, 512, 512
+FLOPS = 2 * J * (3 * K * R + R * N)
+
+F32 = mybir.dt.float32
+BF16 = mybir.dt.bfloat16
+I32 = mybir.dt.int32
+U32 = mybir.dt.uint32
+U16 = mybir.dt.uint16
+U8 = mybir.dt.uint8
+FP8X4 = mybir.dt.float8_e4m3fn_x4
+FP4X4 = mybir.dt.float4_e2m1fn_x4
+ALU = mybir.AluOpType
+ACT = mybir.ActivationFunctionType
+
+P = 128
+PASSES = 2
+TILES = 4
+HALF = J // 2
+H_ON_SCALAR = (0, 1, 2)
+
+
+def tile_moe_expert_hidden_gated_pair_pl_kernel(
+    tc, xt_words, xt_scales, wa_words, wa_scales, wc_words, wc_scales, wg_words, wg_scales,
+    us, wb_words, wb_scales, rw, offs, offs2, out_0, out_1, out_2,
+):
+    nc = tc.nc
+    with ExitStack() as ctx:
+        lists = ctx.enter_context(tc.tile_pool(name="lists", bufs=1))
+        keep = ctx.enter_context(tc.tile_pool(name="keep", bufs=1))
+        psum = ctx.enter_context(tc.psum_pool(name="psum", bufs=2))
+
+        def held(name, shape, dtype):
+            return keep.tile(shape, dtype, name=name, align_bytes=64)
+
+        offs_sb = [lists.tile([P, J // 16], U16, name="offs%d" % l) for l in range(2)]
+        x_words = [held("x_words%d" % z, [P, T], U16) for z in range(PASSES)]
+        x_scales = held("x_scales", [P, PASSES, T], U8)
+        wg_sb = held("wg_sb", [P, PASSES, R], U32)
+        wa_sb = held("wa_sb", [P, PASSES, R], U32)
+        wc_sb = held("wc_sb", [P, PASSES, R], U16)
+        wb_raw = held("wb_raw", [P, N], U16)
+        wg_sc = held("wg_sc", [P, PASSES, R], U8)
+        wa_sc = held("wa_sc", [P, PASSES, R], U8)
+        wc_sc = held("wc_sc", [P, PASSES, R], U8)
+        wb_sc_raw = held("wb_sc_raw", [P, N], U8)
+        us_sb = held("us_sb", [P, 4], F32)
+        rw_sb = held("rw_sb", [P, J], F32)
+        ident = held("ident", [P, P], F32)
+        warm = held("warm", [P, 8], F32)
+
+        for plane in (x_scales, wg_sc, wa_sc, wc_sc):
+            nc.vector.memset(plane[:].rearrange("p z c -> p (z c)").bitcast(I32), 0)
+        nc.vector.memset(wb_sc_raw[:].bitcast(I32), 0)
+        nc.gpsimd.memset(warm[:], 0.0)
+        nc.scalar.activation(warm[:, 4:8], warm[:, 0:4], ACT.Sigmoid)
+        make_identity(nc, ident[:])
+
+        def load_scales(engine, plane, src):
+            for q in range(4):
+                engine.dma_start(
+                    out=plane[32 * q : 32 * q + 4].bitcast(I32),
+                    in_=src[:, 4 * q : 4 * q + 4, :].rearrange("z q c -> q z c").bitcast(I32),
+                )
+
+        nc.sync.dma_start(offs_sb[0][:], offs)
+        nc.sync.dma_start(out=x_words[0][:].bitcast(I32), in_=xt_words[0].bitcast(I32))
+        load_scales(nc.sync, x_scales, xt_scales)
+        nc.sync.dma_start(out=x_words[1][:].bitcast(I32), in_=xt_words[1].bitcast(I32))
+        nc.sync.dma_start(out=wg_sb[:].bitcast(I32), in_=wg_words.rearrange("z p c r -> p z (c r)").bitcast(I32))
+        load_scales(nc.sync, wg_sc, wg_scales)
+        nc.sync.dma_start(offs_sb[1][:], offs2)
+        nc.sync.dma_start(out=wa_sb[:].bitcast(I32), in_=wa_words.rearrange("z p c r -> p z (c r)").bitcast(I32))
+        load_scales(nc.sync, wa_sc, wa_scales)
+        nc.sync.dma_start(out=wc_sb[:].bitcast(I32), in_=wc_words.rearrange("z p c -> p z c").bitcast(I32))
+        load_scales(nc.sync, wc_sc, wc_scales)
+        nc.sync.dma_start(out=us_sb[:], in_=us.rearrange("(p t) o -> p (t o)", t=4))
+        nc.sync.dma_start(out=wb_raw[:].bitcast(I32), in_=wb_words[0].bitcast(I32))
+        for q in range(4):
+            nc.sync.dma_start(
+                out=wb_sc_raw[32 * q : 32 * q + 4, :].bitcast(I32),
+                in_=wb_scales[0, 4 * q : 4 * q + 4, :].bitcast(I32),
+            )
+        nc.sync.dma_start(out=rw_sb[:], in_=rw[0].partition_broadcast(P))
+
+        got_w = {}
+
+        def gather_words(l, z, half):
+            tile = held("got_w%d%d%d" % (l, z, half), [P, HALF], U16)
+            nc.vector.tensor_copy(tile[:], x_words[z][:].indirect(offs_sb[l][:, 16 * half : 16 * half + 16]))
+            got_w[l, z, half] = tile
+
+        got_s = {}
+
+        def gather_scales(l, z, half):
+            tile = held("got_s%d%d%d" % (l, z, half), [P, HALF], U8)
+            nc.vector.tensor_copy(tile[:], x_scales[:, z, :].indirect(offs_sb[l][:, 16 * half : 16 * half + 16]))
+            got_s[l, z, half] = tile
+
+        for half in range(2):
+            for l in range(2):
+                for z in range(PASSES):
+                    gather_words(l, z, half)
+                    gather_scales(l, z, half)
+
+        weights = {"g": (wg_sb, wg_sc, FP8X4, 0), "a": (wa_sb, wa_sc, FP8X4, 0), "b": (wc_sb, wc_sc, FP4X4, 1)}
+        banks = {}
+
+        def first_pass(name, i, z):
+            w_sb, w_sc, w_dt, l = weights[name]
+            if z == 0:
+                banks[name, i] = psum.tile([P, R], F32, name="bank_" + name)
+            local = slice((i % 2) * P, (i % 2 + 1) * P)
+            nc.tensor.matmul_mx(
+                out=banks[name, i][:],
+                lhsT=got_w[l, z, i // 2][:, local].bitcast(FP4X4),
+                lhsT_scale=got_s[l, z, i // 2][:, local],
+                rhs=w_sb[:, z, :].bitcast(w_dt),
+                rhs_scale=w_sc[:, z, :],
+                start=(z == 0),
+                stop=(z == PASSES - 1),
+            )
+
+        def dealt(bank):
+            return bank[:].rearrange("p (m t) -> p t m", t=4)
+
+        gate, term_a, term_b, hid_q, hid_s = {}, {}, {}, {}, {}
+
+        def sigmoid(i):
+            gate[i] = held("gate%d" % i, [P, 4, P], F32)
+            nc.scalar.activation(gate[i][:], dealt(banks["g", i]), ACT.Sigmoid)
+
+        def mix_a(i):
+            term_a[i] = held("term_a%d" % i, [P, 4, P], F32)
+            nc.vector.scalar_tensor_tensor(term_a[i][:], dealt(banks["a", i]), -1.0, gate[i][:], ALU.mult, ALU.mult)
+
+        def mix_b(i):
+            term_b[i] = held("term_b%d" % i, [P, 4, P], F32)
+            nc.vector.scalar_tensor_tensor(term_b[i][:], gate[i][:], 1.0, dealt(banks["b", i]), ALU.subtract, ALU.mult)
+
+        def turn(i):
+            banks["h", i] = psum.tile([P, 4, P], F32, name="bank_late")
+            for n, term in enumerate((term_a[i], term_b[i])):
+                for t in range(4):
+                    nc.tensor.matmul(
+                        banks["h", i][:, t, :], term[:, t, :], ident[:],
+                        start=(n == 0 and t == 0), stop=(n == 1 and t == 3), is_transpose=True,
+                    )
+
+        def weave(engine_copy, dst, src):
+            engine_copy(
+                dst[:].rearrange("p (c i) t -> p c t i", i=4),
+                src[:].rearrange("p t (c i) -> p c t i", i=4),
+            )
+
+        def hidden(i):
+            woven = held("hid_woven%d" % i, [P, P, 4], BF16)
+            if i in H_ON_SCALAR:
+                flat = held("hid_flat%d" % i, [P, 4, P], BF16)
+                for t in range(4):
+                    nc.scalar.activation(flat[:, t, :], banks["h", i][:, t, :], ACT.Copy, scale=us_sb[:, t : t + 1])
+                weave(lambda dst, src: nc.scalar.activation(dst, src, ACT.Copy, scale=-1.0), woven, flat)
+            else:
+                nc.vector.scalar_tensor_tensor(
+                    woven[:],
+                    banks["h", i][:].rearrange("p t j -> p j t"),
+                    -1.0,
+                    us_sb[:].rearrange("p (o t) -> p o t", o=1).to_broadcast([P, P, 4]),
+                    ALU.mult,
+                    ALU.mult,
+                )
+            hid_q[i] = held("hid_q%d" % i, [P, P], U32)
+            hid_s[i] = held("hid_s%d" % i, [P, P], U8)
+            nc.vector.quantize_mx(
+                out=hid_q[i][:].bitcast(FP8X4), scales=hid_s[i][:], in_=woven[:].rearrange("p j t -> p (j t)")
+            )
+
+        dealt_wb = {}
+
+        def deal_wb():
+            dealt_wb["words"] = held("gate0", [P, 4, P], U16)
+            dealt_wb["scales"] = held("gate1", [P, 4, P], U8)
+            nc.vector.tensor_copy(dealt_wb["words"][:], wb_raw[:].rearrange("p (m t) -> p t m", t=4))
+            nc.vector.tensor_copy(dealt_wb["scales"][:], wb_sc_raw[:].rearrange("p (m t) -> p t m", t=4))
+
+        y_codes = held("y_codes", [P, J], U32)
+        y_scales = held("y_scales", [P, J], U8)
+        out_rows = out_0.rearrange("(p t) j -> p t j", t=4)
+        out_words = out_1[0].rearrange("p c r -> p (c r)").bitcast(I32)
+
+        def second(i):
+            banks["p", i] = psum.tile([P, 4, P], F32, name="bank_late")
+            for t in range(4):
+                nc.tensor.matmul_mx(
+                    out=banks["p", i][:, t, :],
+                    lhsT=dealt_wb["words"][:, t, :].bitcast(FP4X4),
+                    lhsT_scale=dealt_wb["scales"][:, t, :],
+                    rhs=hid_q[i][:].bitcast(FP8X4),
+                    rhs_scale=hid_s[i][:],
+                    start=True,
+                    stop=True,
+                )
+
+        def finish(i):
+            slots = slice(i * P, (i + 1) * P)
+            y = held("y%d" % i, [P, 4, P], F32)
+            nc.vector.tensor_tensor(
+                y[:],
+                banks["p", i][:],
+                rw_sb[:, slots].rearrange("p (o j) -> p o j", o=1).to_broadcast([P, 4, P]),
+                ALU.mult,
+            )
+            nc.sync.dma_start(out=out_rows[:, :, slots], in_=y[:])
+            woven = held("y_woven%d" % i, [P, P, 4], BF16)
+            if i == TILES - 1:
+                nc.vector.tensor_tensor(
+                    woven[:],
+                    banks["p", i][:].rearrange("p t j -> p j t"),
+                    rw_sb[:, slots].rearrange("p (j o) -> p j o", o=1).to_broadcast([P, P, 4]),
+                    ALU.mult,
+                )
+            else:
+                weave(nc.scalar.copy, woven, y)
+            nc.vector.quantize_mx(
+                out=y_codes[:, slots].bitcast(FP8X4),
+                scales=y_scales[:, slots],
+                in_=woven[:].rearrange("p j t -> p (j t)"),
+            )
+            nc.sync.dma_start(out=out_words[:, slots], in_=y_codes[:, slots].bitcast(I32))
+
+        def first(name, i):
+            for z in range(PASSES):
+                first_pass(name, i, z)
+
+        for i in (0, 1):
+            first("g", i)
+            sigmoid(i)
+        first("a", 0)
+        first("a", 1)
+        first("b", 0)
+        first("b", 1)
+        for i in (2, 3):
+            first("g", i)
+            sigmoid(i)
+        mix_a(0)
+        mix_a(1)
+        mix_b(0)
+        mix_b(1)
+        first("a", 2)
+        first("b", 2)
+        turn(0)
+        first("a", 3)
+        first("b", 3)
+        turn(1)
+        deal_wb()
+        for i in (2, 3):
+            mix_a(i)
+            mix_b(i)
+        hidden(0)
+        turn(2)
+        hidden(1)
+        second(0)
+        turn(3)
+        second(1)
+        hidden(2)
+        finish(0)
+        hidden(3)
+        second(2)
+        finish(1)
+        second(3)
+        finish(2)
+        finish(3)
+        for q in range(4):
+            engine = nc.sync if q % 2 == 0 else nc.scalar
+            engine.dma_start(
+                out=out_2[0, 4 * q : 4 * q + 4, :].bitcast(I32), in_=y_scales[32 * q : 32 * q + 4, :].bitcast(I32)
+            )

@@ -21,7 +21,10 @@ P = 128
 PASSES = 2
 TILES = 4
 HALF = J // 2
-H_ON_SCALAR = (0, 1, 2)
+H_ON_SCALAR = ()
+A_ON_GPSIMD = (0, 1)
+Y_ON_GPSIMD = ()
+BANK = {"g": (0, 1, 2, 3), "a": (4, 5, 6, 7), "b": (0, 1, 2, 3), "h": (4, 5, 6, 7), "p": (0, 1, 2, 3)}
 
 
 def tile_moe_expert_hidden_gated_pair_pl_kernel(
@@ -32,14 +35,16 @@ def tile_moe_expert_hidden_gated_pair_pl_kernel(
     with ExitStack() as ctx:
         lists = ctx.enter_context(tc.tile_pool(name="lists", bufs=1))
         keep = ctx.enter_context(tc.tile_pool(name="keep", bufs=1))
-        psum = ctx.enter_context(tc.psum_pool(name="psum", bufs=2))
+        overlay = ctx.enter_context(tc.tile_pool(name="overlay", bufs=1))
+        psum = ctx.enter_context(tc.psum_pool(name="psum", bufs=1))
 
         def held(name, shape, dtype):
             return keep.tile(shape, dtype, name=name, align_bytes=64)
 
         offs_sb = [lists.tile([P, J // 16], U16, name="offs%d" % l) for l in range(2)]
         x_words = [held("x_words%d" % z, [P, T], U16) for z in range(PASSES)]
-        x_scales = held("x_scales", [P, PASSES, T], U8)
+        x_scales = held("x_scales", [P, T], U8)
+        moved_sc = [held("moved_sc%d" % l, [P, J], U8) for l in range(2)]
         wg_sb = held("wg_sb", [P, PASSES, R], U32)
         wa_sb = held("wa_sb", [P, PASSES, R], U32)
         wc_sb = held("wc_sb", [P, PASSES, R], U16)
@@ -53,9 +58,11 @@ def tile_moe_expert_hidden_gated_pair_pl_kernel(
         ident = held("ident", [P, P], F32)
         warm = held("warm", [P, 8], F32)
 
-        for plane in (x_scales, wg_sc, wa_sc, wc_sc):
+        nc.vector.memset(x_scales[:].bitcast(I32), 0)
+        for plane in (wg_sc, wa_sc, wc_sc):
             nc.vector.memset(plane[:].rearrange("p z c -> p (z c)").bitcast(I32), 0)
-        nc.vector.memset(wb_sc_raw[:].bitcast(I32), 0)
+        for plane in (wb_sc_raw, moved_sc[0], moved_sc[1]):
+            nc.vector.memset(plane[:].bitcast(I32), 0)
         nc.gpsimd.memset(warm[:], 0.0)
         nc.scalar.activation(warm[:, 4:8], warm[:, 0:4], ACT.Sigmoid)
         make_identity(nc, ident[:])
@@ -68,44 +75,53 @@ def tile_moe_expert_hidden_gated_pair_pl_kernel(
                 )
 
         nc.sync.dma_start(offs_sb[0][:], offs)
+        for q in range(4):
+            nc.sync.dma_start(
+                out=x_scales[32 * q : 32 * q + 8, :].bitcast(I32),
+                in_=xt_scales[:, 4 * q : 4 * q + 4, :].bitcast(I32),
+            )
         nc.sync.dma_start(out=x_words[0][:].bitcast(I32), in_=xt_words[0].bitcast(I32))
-        load_scales(nc.sync, x_scales, xt_scales)
         nc.sync.dma_start(out=x_words[1][:].bitcast(I32), in_=xt_words[1].bitcast(I32))
         nc.sync.dma_start(out=wg_sb[:].bitcast(I32), in_=wg_words.rearrange("z p c r -> p z (c r)").bitcast(I32))
         load_scales(nc.sync, wg_sc, wg_scales)
         nc.sync.dma_start(offs_sb[1][:], offs2)
         nc.sync.dma_start(out=wa_sb[:].bitcast(I32), in_=wa_words.rearrange("z p c r -> p z (c r)").bitcast(I32))
         load_scales(nc.sync, wa_sc, wa_scales)
-        nc.sync.dma_start(out=wc_sb[:].bitcast(I32), in_=wc_words.rearrange("z p c -> p z c").bitcast(I32))
-        load_scales(nc.sync, wc_sc, wc_scales)
-        nc.sync.dma_start(out=us_sb[:], in_=us.rearrange("(p t) o -> p (t o)", t=4))
         nc.sync.dma_start(out=wb_raw[:].bitcast(I32), in_=wb_words[0].bitcast(I32))
         for q in range(4):
             nc.sync.dma_start(
                 out=wb_sc_raw[32 * q : 32 * q + 4, :].bitcast(I32),
                 in_=wb_scales[0, 4 * q : 4 * q + 4, :].bitcast(I32),
             )
+        nc.sync.dma_start(out=wc_sb[:].bitcast(I32), in_=wc_words.rearrange("z p c -> p z c").bitcast(I32))
+        load_scales(nc.sync, wc_sc, wc_scales)
+        nc.sync.dma_start(out=us_sb[:], in_=us.rearrange("(p t) o -> p (t o)", t=4))
         nc.sync.dma_start(out=rw_sb[:], in_=rw[0].partition_broadcast(P))
 
-        got_w = {}
+        got_w, got_s = {}, {}
 
-        def gather_words(l, z, half):
-            tile = held("got_w%d%d%d" % (l, z, half), [P, HALF], U16)
-            nc.vector.tensor_copy(tile[:], x_words[z][:].indirect(offs_sb[l][:, 16 * half : 16 * half + 16]))
-            got_w[l, z, half] = tile
+        def gather_words(l, z, first_tile, tiles):
+            words = held("got_w%d%d%d" % (l, z, first_tile), [P, tiles * P], U16)
+            nc.vector.tensor_copy(words[:], x_words[z][:].indirect(offs_sb[l][:, 8 * first_tile : 8 * (first_tile + tiles)]))
+            for i in range(tiles):
+                got_w[l, z, first_tile + i] = words[:, i * P : (i + 1) * P]
 
-        got_s = {}
+        def gather_scales(l):
+            scales = held("got_s%d" % l, [P, J], U8)
+            nc.vector.tensor_copy(scales[:], x_scales[:].indirect(offs_sb[l][:]))
+            nc.gpsimd.dma_start(out=moved_sc[l][0:112, :].bitcast(I32), in_=scales[4:116, :].bitcast(I32))
+            for i in range(TILES):
+                got_s[l, 0, i] = scales[:, i * P : (i + 1) * P]
+                got_s[l, 1, i] = moved_sc[l][:, i * P : (i + 1) * P]
 
-        def gather_scales(l, z, half):
-            tile = held("got_s%d%d%d" % (l, z, half), [P, HALF], U8)
-            nc.vector.tensor_copy(tile[:], x_scales[:, z, :].indirect(offs_sb[l][:, 16 * half : 16 * half + 16]))
-            got_s[l, z, half] = tile
-
-        for half in range(2):
-            for l in range(2):
-                for z in range(PASSES):
-                    gather_words(l, z, half)
-                    gather_scales(l, z, half)
+        gather_scales(0)
+        gather_words(0, 0, 0, 4)
+        gather_words(0, 1, 0, 4)
+        gather_scales(1)
+        gather_words(1, 0, 0, 2)
+        gather_words(1, 1, 0, 2)
+        gather_words(1, 0, 2, 2)
+        gather_words(1, 1, 2, 2)
 
         weights = {"g": (wg_sb, wg_sc, FP8X4, 0), "a": (wa_sb, wa_sc, FP8X4, 0), "b": (wc_sb, wc_sc, FP4X4, 1)}
         banks = {}
@@ -113,12 +129,11 @@ def tile_moe_expert_hidden_gated_pair_pl_kernel(
         def first_pass(name, i, z):
             w_sb, w_sc, w_dt, l = weights[name]
             if z == 0:
-                banks[name, i] = psum.tile([P, R], F32, name="bank_" + name)
-            local = slice((i % 2) * P, (i % 2 + 1) * P)
+                banks[name, i] = psum.tile([P, R], F32, name="bank%d" % BANK[name][i])
             nc.tensor.matmul_mx(
                 out=banks[name, i][:],
-                lhsT=got_w[l, z, i // 2][:, local].bitcast(FP4X4),
-                lhsT_scale=got_s[l, z, i // 2][:, local],
+                lhsT=got_w[l, z, i].bitcast(FP4X4),
+                lhsT_scale=got_s[l, z, i],
                 rhs=w_sb[:, z, :].bitcast(w_dt),
                 rhs_scale=w_sc[:, z, :],
                 start=(z == 0),
@@ -131,20 +146,28 @@ def tile_moe_expert_hidden_gated_pair_pl_kernel(
         gate, term_a, term_b, hid_q, hid_s = {}, {}, {}, {}, {}
 
         def sigmoid(i):
-            gate[i] = held("gate%d" % i, [P, 4, P], F32)
+            if i == 9:
+                gate[i] = overlay.tile([P, 4, P], F32, name="last_gate", align_bytes=64, offset=0)
+            else:
+                gate[i] = held("gate%d" % i, [P, 4, P], F32)
             nc.scalar.activation(gate[i][:], dealt(banks["g", i]), ACT.Sigmoid)
 
         def mix_a(i):
             term_a[i] = held("term_a%d" % i, [P, 4, P], F32)
-            nc.vector.scalar_tensor_tensor(term_a[i][:], dealt(banks["a", i]), -1.0, gate[i][:], ALU.mult, ALU.mult)
+            if i in A_ON_GPSIMD:
+                neg_a = held("neg_a%d" % i, [P, 4, P], F32)
+                nc.scalar.activation(neg_a[:], dealt(banks["a", i]), ACT.Copy, scale=-1.0)
+                nc.gpsimd.tensor_tensor(term_a[i][:], neg_a[:], gate[i][:], ALU.mult)
+            else:
+                nc.vector.scalar_tensor_tensor(term_a[i][:], dealt(banks["a", i]), -1.0, gate[i][:], ALU.mult, ALU.mult)
 
         def mix_b(i):
             term_b[i] = held("term_b%d" % i, [P, 4, P], F32)
             nc.vector.scalar_tensor_tensor(term_b[i][:], gate[i][:], 1.0, dealt(banks["b", i]), ALU.subtract, ALU.mult)
 
         def turn(i):
-            banks["h", i] = psum.tile([P, 4, P], F32, name="bank_late")
-            for n, term in enumerate((term_a[i], term_b[i])):
+            banks["h", i] = psum.tile([P, 4, P], F32, name="bank%d" % BANK["h"][i])
+            for n, term in enumerate((term_b[i], term_a[i])):
                 for t in range(4):
                     nc.tensor.matmul(
                         banks["h", i][:, t, :], term[:, t, :], ident[:],
@@ -182,8 +205,8 @@ def tile_moe_expert_hidden_gated_pair_pl_kernel(
         dealt_wb = {}
 
         def deal_wb():
-            dealt_wb["words"] = held("gate0", [P, 4, P], U16)
-            dealt_wb["scales"] = held("gate1", [P, 4, P], U8)
+            dealt_wb["words"] = held("wb_sb", [P, 4, P], U16)
+            dealt_wb["scales"] = held("wb_sc", [P, 4, P], U8)
             nc.vector.tensor_copy(dealt_wb["words"][:], wb_raw[:].rearrange("p (m t) -> p t m", t=4))
             nc.vector.tensor_copy(dealt_wb["scales"][:], wb_sc_raw[:].rearrange("p (m t) -> p t m", t=4))
 
@@ -193,7 +216,7 @@ def tile_moe_expert_hidden_gated_pair_pl_kernel(
         out_words = out_1[0].rearrange("p c r -> p (c r)").bitcast(I32)
 
         def second(i):
-            banks["p", i] = psum.tile([P, 4, P], F32, name="bank_late")
+            banks["p", i] = psum.tile([P, 4, P], F32, name="bank%d" % BANK["p"][i])
             for t in range(4):
                 nc.tensor.matmul_mx(
                     out=banks["p", i][:, t, :],
@@ -208,15 +231,16 @@ def tile_moe_expert_hidden_gated_pair_pl_kernel(
         def finish(i):
             slots = slice(i * P, (i + 1) * P)
             y = held("y%d" % i, [P, 4, P], F32)
-            nc.vector.tensor_tensor(
-                y[:],
-                banks["p", i][:],
-                rw_sb[:, slots].rearrange("p (o j) -> p o j", o=1).to_broadcast([P, 4, P]),
-                ALU.mult,
-            )
+            rw_rows = rw_sb[:, slots].rearrange("p (o j) -> p o j", o=1).to_broadcast([P, 4, P])
+            if i in Y_ON_GPSIMD:
+                sums = held("sums%d" % i, [P, 4, P], F32)
+                nc.scalar.copy(sums[:], banks["p", i][:])
+                nc.gpsimd.tensor_tensor(y[:], sums[:], rw_rows, ALU.mult)
+            else:
+                nc.vector.tensor_tensor(y[:], banks["p", i][:], rw_rows, ALU.mult)
             nc.sync.dma_start(out=out_rows[:, :, slots], in_=y[:])
             woven = held("y_woven%d" % i, [P, P, 4], BF16)
-            if i == TILES - 1:
+            if i in ():
                 nc.vector.tensor_tensor(
                     woven[:],
                     banks["p", i][:].rearrange("p t j -> p j t"),
@@ -230,48 +254,57 @@ def tile_moe_expert_hidden_gated_pair_pl_kernel(
                 scales=y_scales[:, slots],
                 in_=woven[:].rearrange("p j t -> p (j t)"),
             )
-            nc.sync.dma_start(out=out_words[:, slots], in_=y_codes[:, slots].bitcast(I32))
+            if i in {1: 0, 3: 2}:
+                done = slice({1: 0, 3: 2}[i] * P, (i + 1) * P)
+                nc.sync.dma_start(out=out_words[:, done], in_=y_codes[:, done].bitcast(I32))
 
         def first(name, i):
             for z in range(PASSES):
                 first_pass(name, i, z)
 
-        for i in (0, 1):
-            first("g", i)
-            sigmoid(i)
+        first_pass("g", 0, 0)
+        first_pass("g", 1, 0)
+        first_pass("g", 2, 0)
+        first_pass("g", 3, 0)
+        first_pass("g", 0, 1)
+        sigmoid(0)
+        first_pass("g", 1, 1)
+        sigmoid(1)
+        first_pass("g", 2, 1)
+        sigmoid(2)
+        first_pass("g", 3, 1)
+        sigmoid(3)
         first("a", 0)
-        first("a", 1)
-        first("b", 0)
-        first("b", 1)
-        for i in (2, 3):
-            first("g", i)
-            sigmoid(i)
         mix_a(0)
+        first("a", 1)
         mix_a(1)
-        mix_b(0)
-        mix_b(1)
         first("a", 2)
-        first("b", 2)
-        turn(0)
+        mix_a(2)
         first("a", 3)
-        first("b", 3)
-        turn(1)
+        mix_a(3)
         deal_wb()
-        for i in (2, 3):
-            mix_a(i)
-            mix_b(i)
+        first("b", 0)
+        mix_b(0)
+        first("b", 1)
+        mix_b(1)
+        first("b", 2)
+        mix_b(2)
+        first("b", 3)
+        mix_b(3)
+        turn(0)
         hidden(0)
-        turn(2)
+        turn(1)
         hidden(1)
         second(0)
-        turn(3)
-        second(1)
+        turn(2)
         hidden(2)
-        finish(0)
+        second(1)
+        turn(3)
         hidden(3)
         second(2)
-        finish(1)
         second(3)
+        finish(0)
+        finish(1)
         finish(2)
         finish(3)
         for q in range(4):

@@ -21,8 +21,8 @@ P = 128
 PASSES = 2
 TILES = 4
 HALF = J // 2
-H_ON_SCALAR = ()
-A_ON_GPSIMD = (0, 1)
+H_ON_SCALAR = (1,)
+A_ON_GPSIMD = ()
 Y_ON_GPSIMD = ()
 BANK = {"g": (0, 1, 2, 3), "a": (4, 5, 6, 7), "b": (0, 1, 2, 3), "h": (4, 5, 6, 7), "p": (0, 1, 2, 3)}
 
@@ -58,7 +58,7 @@ def tile_moe_expert_hidden_gated_pair_pl_kernel(
         ident = held("ident", [P, P], F32)
         warm = held("warm", [P, 8], F32)
 
-        nc.vector.memset(x_scales[:].bitcast(I32), 0)
+        nc.gpsimd.memset(x_scales[:].bitcast(I32), 0)
         for plane in (wg_sc, wa_sc, wc_sc):
             nc.vector.memset(plane[:].rearrange("p z c -> p (z c)").bitcast(I32), 0)
         for plane in (wb_sc_raw, moved_sc[0], moved_sc[1]):
@@ -87,15 +87,15 @@ def tile_moe_expert_hidden_gated_pair_pl_kernel(
         nc.sync.dma_start(offs_sb[1][:], offs2)
         nc.sync.dma_start(out=wa_sb[:].bitcast(I32), in_=wa_words.rearrange("z p c r -> p z (c r)").bitcast(I32))
         load_scales(nc.sync, wa_sc, wa_scales)
+        nc.sync.dma_start(out=wc_sb[:].bitcast(I32), in_=wc_words.rearrange("z p c -> p z c").bitcast(I32))
+        load_scales(nc.sync, wc_sc, wc_scales)
+        nc.sync.dma_start(out=us_sb[:], in_=us.rearrange("(p t) o -> p (t o)", t=4))
         nc.sync.dma_start(out=wb_raw[:].bitcast(I32), in_=wb_words[0].bitcast(I32))
         for q in range(4):
             nc.sync.dma_start(
                 out=wb_sc_raw[32 * q : 32 * q + 4, :].bitcast(I32),
                 in_=wb_scales[0, 4 * q : 4 * q + 4, :].bitcast(I32),
             )
-        nc.sync.dma_start(out=wc_sb[:].bitcast(I32), in_=wc_words.rearrange("z p c -> p z c").bitcast(I32))
-        load_scales(nc.sync, wc_sc, wc_scales)
-        nc.sync.dma_start(out=us_sb[:], in_=us.rearrange("(p t) o -> p (t o)", t=4))
         nc.sync.dma_start(out=rw_sb[:], in_=rw[0].partition_broadcast(P))
 
         got_w, got_s = {}, {}
@@ -109,7 +109,7 @@ def tile_moe_expert_hidden_gated_pair_pl_kernel(
         def gather_scales(l):
             scales = held("got_s%d" % l, [P, J], U8)
             nc.vector.tensor_copy(scales[:], x_scales[:].indirect(offs_sb[l][:]))
-            nc.gpsimd.dma_start(out=moved_sc[l][0:112, :].bitcast(I32), in_=scales[4:116, :].bitcast(I32))
+            nc.scalar.dma_start(out=moved_sc[l][0:112, :].bitcast(I32), in_=scales[4:116, :].bitcast(I32))
             for i in range(TILES):
                 got_s[l, 0, i] = scales[:, i * P : (i + 1) * P]
                 got_s[l, 1, i] = moved_sc[l][:, i * P : (i + 1) * P]
@@ -282,26 +282,26 @@ def tile_moe_expert_hidden_gated_pair_pl_kernel(
         mix_a(2)
         first("a", 3)
         mix_a(3)
-        deal_wb()
         first("b", 0)
-        mix_b(0)
         first("b", 1)
-        mix_b(1)
         first("b", 2)
-        mix_b(2)
         first("b", 3)
+        mix_b(0)
+        mix_b(1)
+        mix_b(2)
         mix_b(3)
+        deal_wb()
         turn(0)
-        hidden(0)
         turn(1)
-        hidden(1)
-        second(0)
         turn(2)
-        hidden(2)
-        second(1)
         turn(3)
-        hidden(3)
+        hidden(0)
+        second(0)
+        hidden(1)
+        second(1)
+        hidden(2)
         second(2)
+        hidden(3)
         second(3)
         finish(0)
         finish(1)

from contextlib import ExitStack

import concourse.mybir as mybir
from concourse.masks import make_identity

K, T, J, R, N = 1024, 1024, 512, 512, 512
FLOPS = 2 * J * (3 * K * R + R * N)

F32 = mybir.dt.float32
BF16 = mybir.dt.bfloat16
I32 = mybir.dt.int32
U32 = mybir.dt.uint32
U16 = mybir.dt.uint16
U8 = mybir.dt.uint8
FP8X4 = mybir.dt.float8_e4m3fn_x4
FP4X4 = mybir.dt.float4_e2m1fn_x4
ALU = mybir.AluOpType
ACT = mybir.ActivationFunctionType

P = 128
PASSES = 2
TILES = 4
HALF = J // 2
H_ON_SCALAR = (1,)
A_ON_GPSIMD = ()
Y_ON_GPSIMD = ()
BANK = {"g": (0, 1, 2, 3), "a": (4, 5, 6, 7), "b": (0, 1, 2, 3), "h": (4, 5, 6, 7), "p": (0, 1, 2, 3)}


def tile_moe_expert_hidden_gated_pair_pl_kernel(
    tc, xt_words, xt_scales, wa_words, wa_scales, wc_words, wc_scales, wg_words, wg_scales,
    us, wb_words, wb_scales, rw, offs, offs2, out_0, out_1, out_2,
):
    nc = tc.nc
    with ExitStack() as ctx:
        lists = ctx.enter_context(tc.tile_pool(name="lists", bufs=1))
        keep = ctx.enter_context(tc.tile_pool(name="keep", bufs=1))
        overlay = ctx.enter_context(tc.tile_pool(name="overlay", bufs=1))
        psum = ctx.enter_context(tc.psum_pool(name="psum", bufs=1))

        def held(name, shape, dtype):
            return keep.tile(shape, dtype, name=name, align_bytes=64)

        offs_sb = [lists.tile([P, J // 16], U16, name="offs%d" % l) for l in range(2)]
        x_words = [held("x_words%d" % z, [P, T], U16) for z in range(PASSES)]
        x_scales = held("x_scales", [P, T], U8)
        moved_sc = [held("moved_sc%d" % l, [P, J], U8) for l in range(2)]
        wg_sb = held("wg_sb", [P, PASSES, R], U32)
        wa_sb = held("wa_sb", [P, PASSES, R], U32)
        wc_sb = held("wc_sb", [P, PASSES, R], U16)
        wb_raw = held("wb_raw", [P, N], U16)
        wg_sc = held("wg_sc", [P, PASSES, R], U8)
        wa_sc = held("wa_sc", [P, PASSES, R], U8)
        wc_sc = held("wc_sc", [P, PASSES, R], U8)
        wb_sc_raw = held("wb_sc_raw", [P, N], U8)
        us_sb = held("us_sb", [P, 4], F32)
        rw_sb = held("rw_sb", [P, J], F32)
        ident = held("ident", [P, P], F32)
        warm = held("warm", [P, 8], F32)

        nc.gpsimd.memset(x_scales[:].bitcast(I32), 0)
        for plane in (wg_sc, wa_sc, wc_sc):
            nc.vector.memset(plane[:].rearrange("p z c -> p (z c)").bitcast(I32), 0)
        for plane in (wb_sc_raw, moved_sc[0], moved_sc[1]):
            nc.vector.memset(plane[:].bitcast(I32), 0)
        nc.gpsimd.memset(warm[:], 0.0)
        nc.scalar.activation(warm[:, 4:8], warm[:, 0:4], ACT.Sigmoid)
        make_identity(nc, ident[:])

        def load_scales(engine, plane, src):
            for q in range(4):
                engine.dma_start(
                    out=plane[32 * q : 32 * q + 4].bitcast(I32),
                    in_=src[:, 4 * q : 4 * q + 4, :].rearrange("z q c -> q z c").bitcast(I32),
                )

        nc.sync.dma_start(offs_sb[0][:], offs)
        for q in range(4):
            nc.sync.dma_start(
                out=x_scales[32 * q : 32 * q + 8, :].bitcast(I32),
                in_=xt_scales[:, 4 * q : 4 * q + 4, :].bitcast(I32),
            )
        nc.sync.dma_start(out=x_words[0][:].bitcast(I32), in_=xt_words[0].bitcast(I32))
        nc.sync.dma_start(out=x_words[1][:].bitcast(I32), in_=xt_words[1].bitcast(I32))
        nc.sync.dma_start(out=wg_sb[:].bitcast(I32), in_=wg_words.rearrange("z p c r -> p z (c r)").bitcast(I32))
        load_scales(nc.sync, wg_sc, wg_scales)
        nc.sync.dma_start(offs_sb[1][:], offs2)
        nc.sync.dma_start(out=wa_sb[:].bitcast(I32), in_=wa_words.rearrange("z p c r -> p z (c r)").bitcast(I32))
        load_scales(nc.sync, wa_sc, wa_scales)
        nc.sync.dma_start(out=wc_sb[:].bitcast(I32), in_=wc_words.rearrange("z p c -> p z c").bitcast(I32))
        load_scales(nc.sync, wc_sc, wc_scales)
        nc.sync.dma_start(out=us_sb[:], in_=us.rearrange("(p t) o -> p (t o)", t=4))
        nc.sync.dma_start(out=wb_raw[:].bitcast(I32), in_=wb_words[0].bitcast(I32))
        for q in range(4):
            nc.sync.dma_start(
                out=wb_sc_raw[32 * q : 32 * q + 4, :].bitcast(I32),
                in_=wb_scales[0, 4 * q : 4 * q + 4, :].bitcast(I32),
            )
        nc.sync.dma_start(out=rw_sb[:], in_=rw[0].partition_broadcast(P))

        got_w, got_s = {}, {}

        def gather_words(l, z, first_tile, tiles):
            words = held("got_w%d%d%d" % (l, z, first_tile), [P, tiles * P], U16)
            nc.vector.tensor_copy(words[:], x_words[z][:].indirect(offs_sb[l][:, 8 * first_tile : 8 * (first_tile + tiles)]))
            for i in range(tiles):
                got_w[l, z, first_tile + i] = words[:, i * P : (i + 1) * P]

        def gather_scales(l):
            scales = held("got_s%d" % l, [P, J], U8)
            nc.vector.tensor_copy(scales[:], x_scales[:].indirect(offs_sb[l][:]))
            nc.scalar.dma_start(out=moved_sc[l][0:112, :].bitcast(I32), in_=scales[4:116, :].bitcast(I32))
            for i in range(TILES):
                got_s[l, 0, i] = scales[:, i * P : (i + 1) * P]
                got_s[l, 1, i] = moved_sc[l][:, i * P : (i + 1) * P]

        gather_scales(0)
        gather_words(0, 0, 0, 4)
        gather_words(0, 1, 0, 4)
        gather_scales(1)
        gather_words(1, 0, 0, 2)
        gather_words(1, 1, 0, 2)
        gather_words(1, 0, 2, 2)
        gather_words(1, 1, 2, 2)

        weights = {"g": (wg_sb, wg_sc, FP8X4, 0), "a": (wa_sb, wa_sc, FP8X4, 0), "b": (wc_sb, wc_sc, FP4X4, 1)}
        banks = {}

        def first_pass(name, i, z):
            w_sb, w_sc, w_dt, l = weights[name]
            if z == 0:
                banks[name, i] = psum.tile([P, R], F32, name="bank%d" % BANK[name][i])
            nc.tensor.matmul_mx(
                out=banks[name, i][:],
                lhsT=got_w[l, z, i].bitcast(FP4X4),
                lhsT_scale=got_s[l, z, i],
                rhs=w_sb[:, z, :].bitcast(w_dt),
                rhs_scale=w_sc[:, z, :],
                start=(z == 0),
                stop=(z == PASSES - 1),
            )

        def dealt(bank):
            return bank[:].rearrange("p (m t) -> p t m", t=4)

        gate, term_a, term_b, hid_q, hid_s = {}, {}, {}, {}, {}

        def sigmoid(i):
            if i == 9:
                gate[i] = overlay.tile([P, 4, P], F32, name="last_gate", align_bytes=64, offset=0)
            else:
                gate[i] = held("gate%d" % i, [P, 4, P], F32)
            nc.scalar.activation(gate[i][:], dealt(banks["g", i]), ACT.Sigmoid)

        def mix_a(i):
            term_a[i] = held("term_a%d" % i, [P, 4, P], F32)
            if i in A_ON_GPSIMD:
                neg_a = held("neg_a%d" % i, [P, 4, P], F32)
                nc.scalar.activation(neg_a[:], dealt(banks["a", i]), ACT.Copy, scale=-1.0)
                nc.gpsimd.tensor_tensor(term_a[i][:], neg_a[:], gate[i][:], ALU.mult)
            else:
                nc.vector.scalar_tensor_tensor(term_a[i][:], dealt(banks["a", i]), -1.0, gate[i][:], ALU.mult, ALU.mult)

        def mix_b(i):
            term_b[i] = held("term_b%d" % i, [P, 4, P], F32)
            nc.vector.scalar_tensor_tensor(term_b[i][:], gate[i][:], 1.0, dealt(banks["b", i]), ALU.subtract, ALU.mult)

        def turn(i):
            banks["h", i] = psum.tile([P, 4, P], F32, name="bank%d" % BANK["h"][i])
            for n, term in enumerate((term_b[i], term_a[i])):
                for t in range(4):
                    nc.tensor.matmul(
                        banks["h", i][:, t, :], term[:, t, :], ident[:],
                        start=(n == 0 and t == 0), stop=(n == 1 and t == 3), is_transpose=True,
                    )

        def weave(engine_copy, dst, src):
            engine_copy(
                dst[:].rearrange("p (c i) t -> p c t i", i=4),
                src[:].rearrange("p t (c i) -> p c t i", i=4),
            )

        def hidden(i):
            woven = held("hid_woven%d" % i, [P, P, 4], BF16)
            if i in H_ON_SCALAR:
                flat = held("hid_flat%d" % i, [P, 4, P], BF16)
                for t in range(4):
                    nc.scalar.activation(flat[:, t, :], banks["h", i][:, t, :], ACT.Copy, scale=us_sb[:, t : t + 1])
                weave(lambda dst, src: nc.scalar.activation(dst, src, ACT.Copy, scale=-1.0), woven, flat)
            else:
                nc.vector.scalar_tensor_tensor(
                    woven[:],
                    banks["h", i][:].rearrange("p t j -> p j t"),
                    -1.0,
                    us_sb[:].rearrange("p (o t) -> p o t", o=1).to_broadcast([P, P, 4]),
                    ALU.mult,
                    ALU.mult,
                )
            hid_q[i] = held("hid_q%d" % i, [P, P], U32)
            hid_s[i] = held("hid_s%d" % i, [P, P], U8)
            nc.vector.quantize_mx(
                out=hid_q[i][:].bitcast(FP8X4), scales=hid_s[i][:], in_=woven[:].rearrange("p j t -> p (j t)")
            )

        dealt_wb = {}

        def deal_wb():
            dealt_wb["words"] = held("wb_sb", [P, 4, P], U16)
            dealt_wb["scales"] = held("wb_sc", [P, 4, P], U8)
            nc.vector.tensor_copy(dealt_wb["words"][:], wb_raw[:].rearrange("p (m t) -> p t m", t=4))
            nc.vector.tensor_copy(dealt_wb["scales"][:], wb_sc_raw[:].rearrange("p (m t) -> p t m", t=4))

        y_codes = held("y_codes", [P, J], U32)
        y_scales = held("y_scales", [P, J], U8)
        out_rows = out_0.rearrange("(p t) j -> p t j", t=4)
        out_words = out_1[0].rearrange("p c r -> p (c r)").bitcast(I32)

        def second(i):
            banks["p", i] = psum.tile([P, 4, P], F32, name="bank%d" % BANK["p"][i])
            for t in range(4):
                nc.tensor.matmul_mx(
                    out=banks["p", i][:, t, :],
                    lhsT=dealt_wb["words"][:, t, :].bitcast(FP4X4),
                    lhsT_scale=dealt_wb["scales"][:, t, :],
                    rhs=hid_q[i][:].bitcast(FP8X4),
                    rhs_scale=hid_s[i][:],
                    start=True,
                    stop=True,
                )

        def finish(i):
            slots = slice(i * P, (i + 1) * P)
            y = held("y%d" % i, [P, 4, P], F32)
            rw_rows = rw_sb[:, slots].rearrange("p (o j) -> p o j", o=1).to_broadcast([P, 4, P])
            if i in Y_ON_GPSIMD:
                sums = held("sums%d" % i, [P, 4, P], F32)
                nc.scalar.copy(sums[:], banks["p", i][:])
                nc.gpsimd.tensor_tensor(y[:], sums[:], rw_rows, ALU.mult)
            else:
                nc.vector.tensor_tensor(y[:], banks["p", i][:], rw_rows, ALU.mult)
            nc.sync.dma_start(out=out_rows[:, :, slots], in_=y[:])
            woven = held("y_woven%d" % i, [P, P, 4], BF16)
            if i in ():
                nc.vector.tensor_tensor(
                    woven[:],
                    banks["p", i][:].rearrange("p t j -> p j t"),
                    rw_sb[:, slots].rearrange("p (j o) -> p j o", o=1).to_broadcast([P, P, 4]),
                    ALU.mult,
                )
            else:
                weave(nc.scalar.copy, woven, y)
            nc.vector.quantize_mx(
                out=y_codes[:, slots].bitcast(FP8X4),
                scales=y_scales[:, slots],
                in_=woven[:].rearrange("p j t -> p (j t)"),
            )
            if i in {1: 0, 3: 2}:
                done = slice({1: 0, 3: 2}[i] * P, (i + 1) * P)
                nc.sync.dma_start(out=out_words[:, done], in_=y_codes[:, done].bitcast(I32))

        def first(name, i):
            for z in range(PASSES):
                first_pass(name, i, z)

        first_pass("g", 0, 0)
        first_pass("g", 1, 0)
        first_pass("g", 2, 0)
        first_pass("g", 3, 0)
        first_pass("g", 0, 1)
        sigmoid(0)
        first_pass("g", 1, 1)
        sigmoid(1)
        first_pass("g", 2, 1)
        sigmoid(2)
        first_pass("g", 3, 1)
        sigmoid(3)
        first("a", 0)
        mix_a(0)
        first("a", 1)
        mix_a(1)
        first("a", 2)
        mix_a(2)
        first("a", 3)
        mix_a(3)
        first("b", 0)
        first("b", 1)
        first("b", 2)
        first("b", 3)
        mix_b(0)
        mix_b(1)
        mix_b(2)
        mix_b(3)
        deal_wb()
        turn(0)
        turn(1)
        turn(2)
        turn(3)
        hidden(0)
        second(0)
        hidden(1)
        second(1)
        hidden(2)
        second(2)
        hidden(3)
        second(3)
        finish(0)
        finish(1)
        finish(2)
        finish(3)
        for q in range(4):
            engine = nc.sync if q % 2 == 0 else nc.scalar
            engine.dma_start(
                out=out_2[0, 4 * q : 4 * q + 4, :].bitcast(I32), in_=y_scales[32 * q : 32 * q + 4, :].bitcast(I32)
            )
